import numpy as np
import ml_dtypes

BF16 = ml_dtypes.bfloat16


def bf(x):
    return np.asarray(x, np.float32).astype(BF16)


def f32(x):
    return np.asarray(x, np.float32)


def f64(x):
    return np.asarray(x).astype(np.float64)


def striped(idx):
    return np.tile(idx.reshape(-1, 16).T, (8, 1))


S, K, M, N, E, Q = 256, 512, 256, 256, 2, 128


def setup_inputs():
    return {"base": bf(np.random.standard_normal((M, S))), "x": bf(np.random.standard_normal((K, N))), "w": bf(np.random.standard_normal((E, K, M)) / np.sqrt(K)), "s": f32(0.5 + np.random.random_sample((M, 1))), "b": f32(0.5 * np.random.standard_normal((M, 1))), "offs": striped(np.random.permutation(S))}


def reference(base, x, w, s, b, offs):
    idx = offs[:16].T.reshape(-1)
    z = f64(base).copy()
    for e in range(E):
        z[:, idx[e * Q : (e + 1) * Q]] += f64(w)[e].T @ f64(x)[:, e * Q : (e + 1) * Q]
    return z * f64(s) + f64(b)

@@ -1,0 +1,77 @@
+import concourse.mybir as mybir
+from concourse.masks import make_identity
+
+BF16, F32, U16 = mybir.dt.bfloat16, mybir.dt.float32, mybir.dt.uint16
+MULT, ADD = mybir.AluOpType.mult, mybir.AluOpType.add
+
+P = 128
+E, K, M, S, N = 2, 512, 256, 256, 256
+PIECE = N // E
+CUT = PIECE // 16
+Q = K // P
+A = M // P
+
+WARM_COLUMNS = 256
+
+FLOPS = 2 * N * K * M
+BYTES = 2 * (M * S + K * N + E * K * M) + 4 * (M * S + 2 * M) + 2 * P * N // 16
+
+
+def tile_scatter_matmul_kernel(tc, base, x, w, s, b, offs, out):
+    nc = tc.nc
+    with (
+        tc.tile_pool(name="held", bufs=1) as held,
+        tc.psum_pool(name="psum", bufs=1) as psum,
+    ):
+        base_sb = held.tile([P, A, S], BF16)
+        offsets = held.tile([P, N // 16], U16)
+        x_sb = held.tile([P, Q, N], BF16)
+        w_sb = [held.tile([P, Q, M], BF16, name=f"w_sb{e}") for e in range(E)]
+        s_sb = held.tile([P, A], F32)
+        b_sb = held.tile([P, A], F32)
+        out_sb = [held.tile([P, S], F32, name=f"out_sb{a}") for a in range(A)]
+        ident = held.tile([P, P], BF16)
+
+        x_rows = x.rearrange("(p q) n -> p q n", p=P)
+        w_rows = w.rearrange("e (p q) m -> e p q m", p=P)
+        halves = (slice(0, Q // 2), slice(Q // 2, Q))
+        nc.sync.dma_start(base_sb[:], base.rearrange("(a p) t -> p a t", p=P))
+        nc.sync.dma_start(offsets[:], offs)
+        for half in halves:
+            nc.sync.dma_start(x_sb[:, half, :], x_rows[:, half, :])
+            nc.sync.dma_start(w_sb[0][:, half, :], w_rows[0, :, half, :])
+        for e in range(1, E):
+            nc.sync.dma_start(w_sb[e][:], w_rows[e])
+        nc.sync.dma_start(s_sb[:], s.rearrange("(a p) o -> p (a o)", p=P))
+        nc.sync.dma_start(b_sb[:], b.rearrange("(a p) o -> p (a o)", p=P))
+
+        zeros = held.tile([P, WARM_COLUMNS], BF16)
+        nc.gpsimd.memset(zeros[:], 0.0)
+        idle_bank = psum.tile([P, WARM_COLUMNS], F32)
+        for i in range(6):
+            nc.tensor.matmul(idle_bank[:], zeros[:, 0:P], zeros[:])
+
+        make_identity(nc, ident[:])
+        windows = [psum.tile([P, S], F32, name=f"window{a}") for a in range(A)]
+        for a in range(A):
+            nc.tensor.matmul(windows[a][:], ident[:], base_sb[:, a, :], start=True, stop=False)
+
+        for e in range(E):
+            places = offsets[:, e * CUT : (e + 1) * CUT]
+            for part in halves if e == 0 else (slice(0, Q),):
+                for a in range(A):
+                    for q in range(part.start, part.stop):
+                        nc.tensor.matmul(
+                            windows[a][:].indirect(places),
+                            w_sb[e][:, q, a * P : (a + 1) * P],
+                            x_sb[:, q, e * PIECE : (e + 1) * PIECE],
+                            start=False,
+                            stop=(e == E - 1 and q == Q - 1),
+                        )
+
+        out_rows = out.rearrange("(a p) t -> p a t", p=P)
+        for a in range(A):
+            nc.vector.tensor_scalar(
+                out_sb[a][:], windows[a][:], s_sb[:, a : a + 1], b_sb[:, a : a + 1], MULT, ADD
+            )
+            nc.sync.dma_start(out_rows[:, a, :], out_sb[a][:])

@@ -1,8 +1,7 @@
 import concourse.mybir as mybir
-from concourse.masks import make_identity
 
 BF16, F32, U16 = mybir.dt.bfloat16, mybir.dt.float32, mybir.dt.uint16
-MULT, ADD = mybir.AluOpType.mult, mybir.AluOpType.add
+MULT, ADD, NOT_EQUAL = mybir.AluOpType.mult, mybir.AluOpType.add, mybir.AluOpType.not_equal
 
 P = 128
 E, K, M, S, N = 2, 512, 256, 256, 256
@@ -11,7 +10,7 @@ CUT = PIECE // 16
 Q = K // P
 A = M // P
 
-WARM_COLUMNS = 256
+WARM_BLOCKS = 3
 
 FLOPS = 2 * N * K * M
 BYTES = 2 * (M * S + K * N + E * K * M) + 4 * (M * S + 2 * M) + 2 * P * N // 16
@@ -35,41 +34,53 @@ def tile_scatter_matmul_kernel(tc, base, x, w, s, b, offs, out):
         x_rows = x.rearrange("(p q) n -> p q n", p=P)
         w_rows = w.rearrange("e (p q) m -> e p q m", p=P)
         halves = (slice(0, Q // 2), slice(Q // 2, Q))
-        nc.sync.dma_start(base_sb[:], base.rearrange("(a p) t -> p a t", p=P))
+        nc.sync.dma_start(base_sb[:], base.rearrange("(p a) t -> p a t", p=P))
         nc.sync.dma_start(offsets[:], offs)
-        for half in halves:
-            nc.sync.dma_start(x_sb[:, half, :], x_rows[:, half, :])
-            nc.sync.dma_start(w_sb[0][:, half, :], w_rows[0, :, half, :])
-        for e in range(1, E):
-            nc.sync.dma_start(w_sb[e][:], w_rows[e])
-        nc.sync.dma_start(s_sb[:], s.rearrange("(a p) o -> p (a o)", p=P))
-        nc.sync.dma_start(b_sb[:], b.rearrange("(a p) o -> p (a o)", p=P))
+        nc.sync.dma_start(x_sb[:, halves[0], :], x_rows[:, halves[0], :])
+        for q in range(Q // 2):
+            nc.sync.dma_start(w_sb[0][:, q, :], w_rows[0, :, q, :])
+        nc.sync.dma_start(w_sb[1][:, halves[0], :], w_rows[1, :, halves[0], :])
+        nc.sync.dma_start(x_sb[:, halves[1], :], x_rows[:, halves[1], :])
+        for e in range(E):
+            nc.sync.dma_start(w_sb[e][:, halves[1], :], w_rows[e, :, halves[1], :])
+        nc.sync.dma_start(s_sb[:], s.rearrange("(p a) o -> p (a o)", p=P))
+        nc.sync.dma_start(b_sb[:], b.rearrange("(p a) o -> p (a o)", p=P))
 
-        zeros = held.tile([P, WARM_COLUMNS], BF16)
-        nc.gpsimd.memset(zeros[:], 0.0)
-        idle_bank = psum.tile([P, WARM_COLUMNS], F32)
-        for i in range(6):
-            nc.tensor.matmul(idle_bank[:], zeros[:, 0:P], zeros[:])
+        zeros = held.tile([P, P], F32)
+        ident_f32 = held.tile([P, P], F32)
+        nc.vector.memset(zeros[:], 0.0)
+        nc.gpsimd.affine_select(
+            out=ident_f32[:], in_=zeros[:], pattern=[[-1, P]], compare_op=NOT_EQUAL,
+            fill=1.0, base=0, channel_multiplier=1,
+        )
+        nc.vector.tensor_copy(ident[:], ident_f32[:])
 
-        make_identity(nc, ident[:])
+        idle_bank = psum.tile([P, WARM_BLOCKS, P], F32)
+        nc.tensor.matmul(idle_bank[:], zeros[:], zeros[:].unsqueeze(1).to_broadcast([P, WARM_BLOCKS, P]))
+
         windows = [psum.tile([P, S], F32, name=f"window{a}") for a in range(A)]
         for a in range(A):
             nc.tensor.matmul(windows[a][:], ident[:], base_sb[:, a, :], start=True, stop=False)
 
-        for e in range(E):
-            places = offsets[:, e * CUT : (e + 1) * CUT]
-            for part in halves if e == 0 else (slice(0, Q),):
-                for a in range(A):
-                    for q in range(part.start, part.stop):
-                        nc.tensor.matmul(
-                            windows[a][:].indirect(places),
-                            w_sb[e][:, q, a * P : (a + 1) * P],
-                            x_sb[:, q, e * PIECE : (e + 1) * PIECE],
-                            start=False,
-                            stop=(e == E - 1 and q == Q - 1),
-                        )
+        def scatter(e, a, q):
+            nc.tensor.matmul(
+                windows[a][:].indirect(offsets[:, e * CUT : (e + 1) * CUT]),
+                w_sb[e][:, q, a::A],
+                x_sb[:, q, e * PIECE : (e + 1) * PIECE],
+                start=False,
+                stop=(e == E - 1 and q == Q - 1),
+            )
 
-        out_rows = out.rearrange("(a p) t -> p a t", p=P)
+        for e in range(E):
+            for q in range(Q // 2):
+                for a in range(A):
+                    scatter(e, a, q)
+        for a in range(A):
+            for e in range(E):
+                for q in range(Q // 2, Q):
+                    scatter(e, a, q)
+
+        out_rows = out.rearrange("(p a) t -> p a t", p=P)
         for a in range(A):
             nc.vector.tensor_scalar(
                 out_sb[a][:], windows[a][:], s_sb[:, a : a + 1], b_sb[:, a : a + 1], MULT, ADD

@@ -82,7 +82,8 @@ def tile_scatter_matmul_kernel(tc, base, x, w, s, b, offs, out):
 
         out_rows = out.rearrange("(p a) t -> p a t", p=P)
         for a in range(A):
-            nc.vector.tensor_scalar(
-                out_sb[a][:], windows[a][:], s_sb[:, a : a + 1], b_sb[:, a : a + 1], MULT, ADD
-            )
-            nc.sync.dma_start(out_rows[:, a, :], out_sb[a][:])
+            for cols in (slice(0, S // 2), slice(S // 2, S)) if a == A - 1 else (slice(0, S),):
+                nc.vector.tensor_scalar(
+                    out_sb[a][:, cols], windows[a][:, cols], s_sb[:, a : a + 1], b_sb[:, a : a + 1], MULT, ADD
+                )
+                nc.sync.dma_start(out_rows[:, a, cols], out_sb[a][:, cols])

@@ -10,6 +10,8 @@ CUT = PIECE // 16
 Q = K // P
 A = M // P
 
+ROW_ALIGN = 512
+
 WARM_BLOCKS = 3
 
 FLOPS = 2 * N * K * M
@@ -22,13 +24,13 @@ def tile_scatter_matmul_kernel(tc, base, x, w, s, b, offs, out):
         tc.tile_pool(name="held", bufs=1) as held,
         tc.psum_pool(name="psum", bufs=1) as psum,
     ):
-        base_sb = held.tile([P, A, S], BF16)
+        base_sb = held.tile([P, A, S], BF16, align_bytes=ROW_ALIGN)
         offsets = held.tile([P, N // 16], U16)
-        x_sb = held.tile([P, Q, N], BF16)
-        w_sb = [held.tile([P, Q, M], BF16, name=f"w_sb{e}") for e in range(E)]
+        x_sb = held.tile([P, Q, N], BF16, align_bytes=ROW_ALIGN)
+        w_sb = [held.tile([P, Q, M], BF16, name=f"w_sb{e}", align_bytes=ROW_ALIGN) for e in range(E)]
         s_sb = held.tile([P, A], F32)
         b_sb = held.tile([P, A], F32)
-        out_sb = [held.tile([P, S], F32, name=f"out_sb{a}") for a in range(A)]
+        out_sb = [held.tile([P, S], F32, name=f"out_sb{a}", align_bytes=ROW_ALIGN) for a in range(A)]
         ident = held.tile([P, P], BF16)
 
         x_rows = x.rearrange("(p q) n -> p q n", p=P)

@@ -12,7 +12,9 @@ A = M // P
 
 ROW_ALIGN = 512
 
-WARM_BLOCKS = 3
+WARM_SEED = 32
+WARM_BLOCKS = 12
+WARM_TILES = 2
 
 FLOPS = 2 * N * K * M
 BYTES = 2 * (M * S + K * N + E * K * M) + 4 * (M * S + 2 * M) + 2 * P * N // 16
@@ -48,6 +50,16 @@ def tile_scatter_matmul_kernel(tc, base, x, w, s, b, offs, out):
         nc.sync.dma_start(s_sb[:], s.rearrange("(p a) o -> p (a o)", p=P))
         nc.sync.dma_start(b_sb[:], b.rearrange("(p a) o -> p (a o)", p=P))
 
+        seed = held.tile([P, WARM_SEED], F32)
+        nc.gpsimd.memset(seed[:], 0.0)
+        idle_bank = psum.tile([P, WARM_BLOCKS, WARM_SEED], F32)
+        for c in range(WARM_TILES):
+            nc.tensor.matmul(
+                idle_bank[c * WARM_SEED : (c + 1) * WARM_SEED],
+                seed[:],
+                seed[:].unsqueeze(1).to_broadcast([P, WARM_BLOCKS, WARM_SEED]),
+            )
+
         zeros = held.tile([P, P], F32)
         ident_f32 = held.tile([P, P], F32)
         nc.vector.memset(zeros[:], 0.0)
@@ -56,9 +68,6 @@ def tile_scatter_matmul_kernel(tc, base, x, w, s, b, offs, out):
             fill=1.0, base=0, channel_multiplier=1,
         )
         nc.vector.tensor_copy(ident[:], ident_f32[:])
-
-        idle_bank = psum.tile([P, WARM_BLOCKS, P], F32)
-        nc.tensor.matmul(idle_bank[:], zeros[:], zeros[:].unsqueeze(1).to_broadcast([P, WARM_BLOCKS, P]))
 
         windows = [psum.tile([P, S], F32, name=f"window{a}") for a in range(A)]
         for a in range(A):

@@ -14,7 +14,6 @@ ROW_ALIGN = 512
 
 WARM_SEED = 32
 WARM_BLOCKS = 12
-WARM_TILES = 2
 
 FLOPS = 2 * N * K * M
 BYTES = 2 * (M * S + K * N + E * K * M) + 4 * (M * S + 2 * M) + 2 * P * N // 16
@@ -35,30 +34,25 @@ def tile_scatter_matmul_kernel(tc, base, x, w, s, b, offs, out):
         out_sb = [held.tile([P, S], F32, name=f"out_sb{a}", align_bytes=ROW_ALIGN) for a in range(A)]
         ident = held.tile([P, P], BF16)
 
-        x_rows = x.rearrange("(p q) n -> p q n", p=P)
-        w_rows = w.rearrange("e (p q) m -> e p q m", p=P)
+        x_rows = x.rearrange("(h p j) n -> h p j n", p=P, j=Q // 2)
+        w_rows = w.rearrange("e (h p j) m -> e h p j m", p=P, j=Q // 2)
         halves = (slice(0, Q // 2), slice(Q // 2, Q))
         nc.sync.dma_start(base_sb[:], base.rearrange("(p a) t -> p a t", p=P))
         nc.sync.dma_start(offsets[:], offs)
-        nc.sync.dma_start(x_sb[:, halves[0], :], x_rows[:, halves[0], :])
+        nc.sync.dma_start(x_sb[:, halves[0], :], x_rows[0])
         for q in range(Q // 2):
-            nc.sync.dma_start(w_sb[0][:, q, :], w_rows[0, :, q, :])
-        nc.sync.dma_start(w_sb[1][:, halves[0], :], w_rows[1, :, halves[0], :])
-        nc.sync.dma_start(x_sb[:, halves[1], :], x_rows[:, halves[1], :])
+            nc.sync.dma_start(w_sb[0][:, q, :], w_rows[0, 0, :, q, :])
+        nc.sync.dma_start(w_sb[1][:, halves[0], :], w_rows[1, 0])
+        nc.sync.dma_start(x_sb[:, halves[1], :], x_rows[1])
         for e in range(E):
-            nc.sync.dma_start(w_sb[e][:, halves[1], :], w_rows[e, :, halves[1], :])
+            nc.sync.dma_start(w_sb[e][:, halves[1], :], w_rows[e, 1])
         nc.sync.dma_start(s_sb[:], s.rearrange("(p a) o -> p (a o)", p=P))
         nc.sync.dma_start(b_sb[:], b.rearrange("(p a) o -> p (a o)", p=P))
 
         seed = held.tile([P, WARM_SEED], F32)
         nc.gpsimd.memset(seed[:], 0.0)
-        idle_bank = psum.tile([P, WARM_BLOCKS, WARM_SEED], F32)
-        for c in range(WARM_TILES):
-            nc.tensor.matmul(
-                idle_bank[c * WARM_SEED : (c + 1) * WARM_SEED],
-                seed[:],
-                seed[:].unsqueeze(1).to_broadcast([P, WARM_BLOCKS, WARM_SEED]),
-            )
+        idle_bank = psum.tile([WARM_SEED, WARM_BLOCKS, WARM_SEED], F32)
+        nc.tensor.matmul(idle_bank[:], seed[:], seed[:].unsqueeze(1).to_broadcast([P, WARM_BLOCKS, WARM_SEED]))
 
         zeros = held.tile([P, P], F32)
         ident_f32 = held.tile([P, P], F32)

@@ -44,8 +44,9 @@ def tile_scatter_matmul_kernel(tc, base, x, w, s, b, offs, out):
             nc.sync.dma_start(w_sb[0][:, q, :], w_rows[0, 0, :, q, :])
         nc.sync.dma_start(w_sb[1][:, halves[0], :], w_rows[1, 0])
         nc.sync.dma_start(x_sb[:, halves[1], :], x_rows[1])
-        for e in range(E):
-            nc.sync.dma_start(w_sb[e][:, halves[1], :], w_rows[e, 1])
+        nc.sync.dma_start(w_sb[0][:, halves[1], :], w_rows[0, 1])
+        for j in range(Q // 2):
+            nc.sync.dma_start(w_sb[1][:, Q // 2 + j, :], w_rows[1, 1, :, j, :])
         nc.sync.dma_start(s_sb[:], s.rearrange("(p a) o -> p (a o)", p=P))
         nc.sync.dma_start(b_sb[:], b.rearrange("(p a) o -> p (a o)", p=P))
 
@@ -87,7 +88,7 @@ def tile_scatter_matmul_kernel(tc, base, x, w, s, b, offs, out):
 
         out_rows = out.rearrange("(p a) t -> p a t", p=P)
         for a in range(A):
-            for cols in (slice(0, S // 2), slice(S // 2, S)) if a == A - 1 else (slice(0, S),):
+            for cols in (slice(0, S // 2), slice(S // 2, S)):
                 nc.vector.tensor_scalar(
                     out_sb[a][:, cols], windows[a][:, cols], s_sb[:, a : a + 1], b_sb[:, a : a + 1], MULT, ADD
                 )

@@ -34,19 +34,17 @@ def tile_scatter_matmul_kernel(tc, base, x, w, s, b, offs, out):
         out_sb = [held.tile([P, S], F32, name=f"out_sb{a}", align_bytes=ROW_ALIGN) for a in range(A)]
         ident = held.tile([P, P], BF16)
 
-        x_rows = x.rearrange("(h p j) n -> h p j n", p=P, j=Q // 2)
-        w_rows = w.rearrange("e (h p j) m -> e h p j m", p=P, j=Q // 2)
-        halves = (slice(0, Q // 2), slice(Q // 2, Q))
+        x_rows = x.rearrange("(p q) n -> p q n", p=P)
+        w_rows = w.rearrange("e (p q) m -> e p q m", p=P)
         nc.sync.dma_start(base_sb[:], base.rearrange("(p a) t -> p a t", p=P))
         nc.sync.dma_start(offsets[:], offs)
-        nc.sync.dma_start(x_sb[:, halves[0], :], x_rows[0])
-        for q in range(Q // 2):
-            nc.sync.dma_start(w_sb[0][:, q, :], w_rows[0, 0, :, q, :])
-        nc.sync.dma_start(w_sb[1][:, halves[0], :], w_rows[1, 0])
-        nc.sync.dma_start(x_sb[:, halves[1], :], x_rows[1])
-        nc.sync.dma_start(w_sb[0][:, halves[1], :], w_rows[0, 1])
-        for j in range(Q // 2):
-            nc.sync.dma_start(w_sb[1][:, Q // 2 + j, :], w_rows[1, 1, :, j, :])
+        first, middle, last = slice(0, 1), slice(1, Q - 1), slice(Q - 1, Q)
+        early, late = slice(0, Q // 2), slice(Q // 2, Q)
+        for step, half in ((first, early), (middle, None), (last, late)):
+            nc.sync.dma_start(x_sb[:, step, :], x_rows[:, step, :])
+            nc.sync.dma_start(w_sb[0][:, step, :], w_rows[0, :, step, :])
+            if half is not None:
+                nc.sync.dma_start(w_sb[1][:, half, :], w_rows[1, :, half, :])
         nc.sync.dma_start(s_sb[:], s.rearrange("(p a) o -> p (a o)", p=P))
         nc.sync.dma_start(b_sb[:], b.rearrange("(p a) o -> p (a o)", p=P))
 
@@ -77,13 +75,16 @@ def tile_scatter_matmul_kernel(tc, base, x, w, s, b, offs, out):
                 stop=(e == E - 1 and q == Q - 1),
             )
 
-        for e in range(E):
-            for q in range(Q // 2):
+        def blocks(part):
+            return range(part.start, part.stop)
+
+        for e, part in ((0, first), (1, early), (0, middle)):
+            for q in blocks(part):
                 for a in range(A):
                     scatter(e, a, q)
         for a in range(A):
-            for e in range(E):
-                for q in range(Q // 2, Q):
+            for e, part in ((0, last), (1, late)):
+                for q in blocks(part):
                     scatter(e, a, q)
 
         out_rows = out.rearrange("(p a) t -> p a t", p=P)

@@ -12,8 +12,8 @@ A = M // P
 
 ROW_ALIGN = 512
 
-WARM_SEED = 32
-WARM_BLOCKS = 12
+WARM_SEED = 8
+WARM_BLOCKS = 33
 
 FLOPS = 2 * N * K * M
 BYTES = 2 * (M * S + K * N + E * K * M) + 4 * (M * S + 2 * M) + 2 * P * N // 16

@@ -1,7 +1,7 @@
 import concourse.mybir as mybir
 
 BF16, F32, U16 = mybir.dt.bfloat16, mybir.dt.float32, mybir.dt.uint16
-MULT, ADD, NOT_EQUAL = mybir.AluOpType.mult, mybir.AluOpType.add, mybir.AluOpType.not_equal
+MULT, ADD, IS_EQUAL = mybir.AluOpType.mult, mybir.AluOpType.add, mybir.AluOpType.is_equal
 
 P = 128
 E, K, M, S, N = 2, 512, 256, 256, 256
@@ -13,7 +13,7 @@ A = M // P
 ROW_ALIGN = 512
 
 WARM_SEED = 8
-WARM_BLOCKS = 33
+WARM_BLOCKS = 40
 
 FLOPS = 2 * N * K * M
 BYTES = 2 * (M * S + K * N + E * K * M) + 4 * (M * S + 2 * M) + 2 * P * N // 16
@@ -53,14 +53,11 @@ def tile_scatter_matmul_kernel(tc, base, x, w, s, b, offs, out):
         idle_bank = psum.tile([WARM_SEED, WARM_BLOCKS, WARM_SEED], F32)
         nc.tensor.matmul(idle_bank[:], seed[:], seed[:].unsqueeze(1).to_broadcast([P, WARM_BLOCKS, WARM_SEED]))
 
-        zeros = held.tile([P, P], F32)
-        ident_f32 = held.tile([P, P], F32)
-        nc.vector.memset(zeros[:], 0.0)
-        nc.gpsimd.affine_select(
-            out=ident_f32[:], in_=zeros[:], pattern=[[-1, P]], compare_op=NOT_EQUAL,
-            fill=1.0, base=0, channel_multiplier=1,
+        distance = held.tile([P, P], F32)
+        nc.gpsimd.iota(
+            distance[:], pattern=[[1, P]], base=0, channel_multiplier=-1, allow_small_or_imprecise_dtypes=True
         )
-        nc.vector.tensor_copy(ident[:], ident_f32[:])
+        nc.vector.tensor_scalar(ident[:], distance[:], 0.0, None, IS_EQUAL)
 
         windows = [psum.tile([P, S], F32, name=f"window{a}") for a in range(A)]
         for a in range(A):

@@ -12,8 +12,7 @@ A = M // P
 
 ROW_ALIGN = 512
 
-WARM_SEED = 8
-WARM_BLOCKS = 40
+WARM_COLUMNS = 320
 
 FLOPS = 2 * N * K * M
 BYTES = 2 * (M * S + K * N + E * K * M) + 4 * (M * S + 2 * M) + 2 * P * N // 16
@@ -34,24 +33,34 @@ def tile_scatter_matmul_kernel(tc, base, x, w, s, b, offs, out):
         out_sb = [held.tile([P, S], F32, name=f"out_sb{a}", align_bytes=ROW_ALIGN) for a in range(A)]
         ident = held.tile([P, P], BF16)
 
-        x_rows = x.rearrange("(p q) n -> p q n", p=P)
-        w_rows = w.rearrange("e (p q) m -> e p q m", p=P)
+        x_blocks = x.rearrange("(p q) n -> p q n", p=P)
+        w_blocks = w.rearrange("e (p q) m -> e p q m", p=P)
+
+        def load_x(blocks):
+            nc.sync.dma_start(x_sb[:, blocks, :], x_blocks[:, blocks, :])
+
+        def load_w(e, blocks):
+            nc.sync.dma_start(w_sb[e][:, blocks, :], w_blocks[e, :, blocks, :])
+
         nc.sync.dma_start(base_sb[:], base.rearrange("(p a) t -> p a t", p=P))
         nc.sync.dma_start(offsets[:], offs)
         first, middle, last = slice(0, 1), slice(1, Q - 1), slice(Q - 1, Q)
         early, late = slice(0, Q // 2), slice(Q // 2, Q)
-        for step, half in ((first, early), (middle, None), (last, late)):
-            nc.sync.dma_start(x_sb[:, step, :], x_rows[:, step, :])
-            nc.sync.dma_start(w_sb[0][:, step, :], w_rows[0, :, step, :])
-            if half is not None:
-                nc.sync.dma_start(w_sb[1][:, half, :], w_rows[1, :, half, :])
+        load_x(first)
+        load_w(0, first)
+        load_w(1, early)
+        load_x(middle)
+        load_w(0, middle)
+        load_x(last)
+        load_w(0, last)
+        load_w(1, late)
         nc.sync.dma_start(s_sb[:], s.rearrange("(p a) o -> p (a o)", p=P))
         nc.sync.dma_start(b_sb[:], b.rearrange("(p a) o -> p (a o)", p=P))
 
-        seed = held.tile([P, WARM_SEED], F32)
-        nc.gpsimd.memset(seed[:], 0.0)
-        idle_bank = psum.tile([WARM_SEED, WARM_BLOCKS, WARM_SEED], F32)
-        nc.tensor.matmul(idle_bank[:], seed[:], seed[:].unsqueeze(1).to_broadcast([P, WARM_BLOCKS, WARM_SEED]))
+        seed = held.tile([P, 1], F32)
+        nc.vector.memset(seed[:], 0.0)
+        idle_bank = psum.tile([1, WARM_COLUMNS], F32)
+        nc.tensor.matmul(idle_bank[:], seed[:], seed[:].to_broadcast([P, WARM_COLUMNS]))
 
         distance = held.tile([P, P], F32)
         nc.gpsimd.iota(
@@ -72,16 +81,13 @@ def tile_scatter_matmul_kernel(tc, base, x, w, s, b, offs, out):
                 stop=(e == E - 1 and q == Q - 1),
             )
 
-        def blocks(part):
-            return range(part.start, part.stop)
-
         for e, part in ((0, first), (1, early), (0, middle)):
-            for q in blocks(part):
+            for q in range(part.start, part.stop):
                 for a in range(A):
                     scatter(e, a, q)
         for a in range(A):
             for e, part in ((0, last), (1, late)):
-                for q in blocks(part):
+                for q in range(part.start, part.stop):
                     scatter(e, a, q)
 
         out_rows = out.rearrange("(p a) t -> p a t", p=P)

@@ -53,7 +53,8 @@ def tile_scatter_matmul_kernel(tc, base, x, w, s, b, offs, out):
         load_w(0, middle)
         load_x(last)
         load_w(0, last)
-        load_w(1, late)
+        for q in range(late.start, late.stop):
+            load_w(1, slice(q, q + 1))
         nc.sync.dma_start(s_sb[:], s.rearrange("(p a) o -> p (a o)", p=P))
         nc.sync.dma_start(b_sb[:], b.rearrange("(p a) o -> p (a o)", p=P))
 
@@ -91,8 +92,9 @@ def tile_scatter_matmul_kernel(tc, base, x, w, s, b, offs, out):
                     scatter(e, a, q)
 
         out_rows = out.rearrange("(p a) t -> p a t", p=P)
+        whole, halves = (slice(0, S),), (slice(0, S // 2), slice(S // 2, S))
         for a in range(A):
-            for cols in (slice(0, S // 2), slice(S // 2, S)):
+            for cols in whole if a == A - 1 else halves:
                 nc.vector.tensor_scalar(
                     out_sb[a][:, cols], windows[a][:, cols], s_sb[:, a : a + 1], b_sb[:, a : a + 1], MULT, ADD
                 )

@@ -9,6 +9,8 @@ PIECE = N // E
 CUT = PIECE // 16
 Q = K // P
 A = M // P
+PAIR = 2
+LAST_STEPS = 3
 
 ROW_ALIGN = 512
 
@@ -44,17 +46,11 @@ def tile_scatter_matmul_kernel(tc, base, x, w, s, b, offs, out):
 
         nc.sync.dma_start(base_sb[:], base.rearrange("(p a) t -> p a t", p=P))
         nc.sync.dma_start(offsets[:], offs)
-        first, middle, last = slice(0, 1), slice(1, Q - 1), slice(Q - 1, Q)
-        early, late = slice(0, Q // 2), slice(Q // 2, Q)
-        load_x(first)
-        load_w(0, first)
-        load_w(1, early)
-        load_x(middle)
-        load_w(0, middle)
-        load_x(last)
-        load_w(0, last)
-        for q in range(late.start, late.stop):
-            load_w(1, slice(q, q + 1))
+        for q in range(Q):
+            load_x(slice(q, q + 1))
+            if q == 0:
+                load_w(0, slice(0, 1))
+            load_w((q + 1) % E, slice(q, min(q + PAIR, Q)))
         nc.sync.dma_start(s_sb[:], s.rearrange("(p a) o -> p (a o)", p=P))
         nc.sync.dma_start(b_sb[:], b.rearrange("(p a) o -> p (a o)", p=P))
 
@@ -73,23 +69,23 @@ def tile_scatter_matmul_kernel(tc, base, x, w, s, b, offs, out):
         for a in range(A):
             nc.tensor.matmul(windows[a][:], ident[:], base_sb[:, a, :], start=True, stop=False)
 
+        steps = [(e, q) for q in range(Q) for e in (q % E, (q + 1) % E)]
+
         def scatter(e, a, q):
             nc.tensor.matmul(
                 windows[a][:].indirect(offsets[:, e * CUT : (e + 1) * CUT]),
                 w_sb[e][:, q, a::A],
                 x_sb[:, q, e * PIECE : (e + 1) * PIECE],
                 start=False,
-                stop=(e == E - 1 and q == Q - 1),
+                stop=((e, q) == steps[-1]),
             )
 
-        for e, part in ((0, first), (1, early), (0, middle)):
-            for q in range(part.start, part.stop):
-                for a in range(A):
-                    scatter(e, a, q)
+        for e, q in steps[:-LAST_STEPS]:
+            for a in range(A):
+                scatter(e, a, q)
         for a in range(A):
-            for e, part in ((0, last), (1, late)):
-                for q in range(part.start, part.stop):
-                    scatter(e, a, q)
+            for e, q in steps[-LAST_STEPS:]:
+                scatter(e, a, q)
 
         out_rows = out.rearrange("(p a) t -> p a t", p=P)
         whole, halves = (slice(0, S),), (slice(0, S // 2), slice(S // 2, S))

@@ -10,7 +10,8 @@ CUT = PIECE // 16
 Q = K // P
 A = M // P
 PAIR = 2
-LAST_STEPS = 3
+LAST_STEPS = 4
+LEAD_COLUMNS = 64
 
 ROW_ALIGN = 512
 
@@ -88,9 +89,9 @@ def tile_scatter_matmul_kernel(tc, base, x, w, s, b, offs, out):
                 scatter(e, a, q)
 
         out_rows = out.rearrange("(p a) t -> p a t", p=P)
-        whole, halves = (slice(0, S),), (slice(0, S // 2), slice(S // 2, S))
+        whole, pieces = (slice(0, S),), (slice(0, LEAD_COLUMNS), slice(LEAD_COLUMNS, S))
         for a in range(A):
-            for cols in whole if a == A - 1 else halves:
+            for cols in pieces if a == A - 1 else whole:
                 nc.vector.tensor_scalar(
                     out_sb[a][:, cols], windows[a][:, cols], s_sb[:, a : a + 1], b_sb[:, a : a + 1], MULT, ADD
                 )

@@ -9,8 +9,7 @@ PIECE = N // E
 CUT = PIECE // 16
 Q = K // P
 A = M // P
-PAIR = 2
-LAST_STEPS = 4
+HALF = Q // 2
 LEAD_COLUMNS = 64
 
 ROW_ALIGN = 512
@@ -29,8 +28,10 @@ def tile_scatter_matmul_kernel(tc, base, x, w, s, b, offs, out):
     ):
         base_sb = held.tile([P, A, S], BF16, align_bytes=ROW_ALIGN)
         offsets = held.tile([P, N // 16], U16)
-        x_sb = held.tile([P, Q, N], BF16, align_bytes=ROW_ALIGN)
-        w_sb = [held.tile([P, Q, M], BF16, name=f"w_sb{e}", align_bytes=ROW_ALIGN) for e in range(E)]
+        x_early = [held.tile([P, HALF, PIECE], BF16, name=f"x_early{e}", align_bytes=ROW_ALIGN) for e in range(E)]
+        x_late = held.tile([P, HALF, N], BF16, align_bytes=ROW_ALIGN)
+        w_first = held.tile([P, Q, M], BF16, align_bytes=ROW_ALIGN)
+        w_second = [held.tile([P, Q, P], BF16, name=f"w_second{a}", align_bytes=ROW_ALIGN) for a in range(A)]
         s_sb = held.tile([P, A], F32)
         b_sb = held.tile([P, A], F32)
         out_sb = [held.tile([P, S], F32, name=f"out_sb{a}", align_bytes=ROW_ALIGN) for a in range(A)]
@@ -39,21 +40,24 @@ def tile_scatter_matmul_kernel(tc, base, x, w, s, b, offs, out):
         x_blocks = x.rearrange("(p q) n -> p q n", p=P)
         w_blocks = w.rearrange("e (p q) m -> e p q m", p=P)
 
-        def load_x(blocks):
-            nc.sync.dma_start(x_sb[:, blocks, :], x_blocks[:, blocks, :])
+        def columns(i):
+            return slice(i * P, (i + 1) * P)
 
-        def load_w(e, blocks):
-            nc.sync.dma_start(w_sb[e][:, blocks, :], w_blocks[e, :, blocks, :])
+        def load_first(blocks):
+            nc.sync.dma_start(w_first[:, blocks, :], w_blocks[0, :, blocks, :])
 
-        nc.sync.dma_start(base_sb[:], base.rearrange("(p a) t -> p a t", p=P))
+        nc.sync.dma_start(base_sb[:], base.rearrange("(a p) t -> p a t", p=P))
         nc.sync.dma_start(offsets[:], offs)
-        for q in range(Q):
-            load_x(slice(q, q + 1))
-            if q == 0:
-                load_w(0, slice(0, 1))
-            load_w((q + 1) % E, slice(q, min(q + PAIR, Q)))
-        nc.sync.dma_start(s_sb[:], s.rearrange("(p a) o -> p (a o)", p=P))
-        nc.sync.dma_start(b_sb[:], b.rearrange("(p a) o -> p (a o)", p=P))
+        nc.sync.dma_start(x_early[0][:], x_blocks[:, :HALF, columns(0)])
+        load_first(slice(0, 1))
+        load_first(slice(1, Q - 1))
+        nc.sync.dma_start(x_late[:], x_blocks[:, HALF:, :])
+        load_first(slice(Q - 1, Q))
+        nc.sync.dma_start(w_second[0][:], w_blocks[1, :, :, columns(0)])
+        nc.sync.dma_start(x_early[1][:], x_blocks[:, :HALF, columns(1)])
+        nc.sync.dma_start(w_second[1][:], w_blocks[1, :, :, columns(1)])
+        nc.sync.dma_start(s_sb[:], s.rearrange("(a p) o -> p (a o)", p=P))
+        nc.sync.dma_start(b_sb[:], b.rearrange("(a p) o -> p (a o)", p=P))
 
         seed = held.tile([P, 1], F32)
         nc.vector.memset(seed[:], 0.0)
@@ -70,28 +74,27 @@ def tile_scatter_matmul_kernel(tc, base, x, w, s, b, offs, out):
         for a in range(A):
             nc.tensor.matmul(windows[a][:], ident[:], base_sb[:, a, :], start=True, stop=False)
 
-        steps = [(e, q) for q in range(Q) for e in (q % E, (q + 1) % E)]
+        second_order = [*range(HALF, Q), *range(HALF)]
 
-        def scatter(e, a, q):
+        def scatter(e, a, q, last=False):
             nc.tensor.matmul(
                 windows[a][:].indirect(offsets[:, e * CUT : (e + 1) * CUT]),
-                w_sb[e][:, q, a::A],
-                x_sb[:, q, e * PIECE : (e + 1) * PIECE],
+                w_first[:, q, columns(a)] if e == 0 else w_second[a][:, q, :],
+                x_early[e][:, q, :] if q < HALF else x_late[:, q - HALF, columns(e)],
                 start=False,
-                stop=((e, q) == steps[-1]),
+                stop=last,
             )
 
-        for e, q in steps[:-LAST_STEPS]:
+        for q in range(Q):
             for a in range(A):
-                scatter(e, a, q)
+                scatter(0, a, q)
         for a in range(A):
-            for e, q in steps[-LAST_STEPS:]:
-                scatter(e, a, q)
+            for q in second_order:
+                scatter(1, a, q, last=(q == second_order[-1]))
 
-        out_rows = out.rearrange("(p a) t -> p a t", p=P)
-        whole, pieces = (slice(0, S),), (slice(0, LEAD_COLUMNS), slice(LEAD_COLUMNS, S))
-        for a in range(A):
-            for cols in pieces if a == A - 1 else whole:
+        out_rows = out.rearrange("(a p) t -> p a t", p=P)
+        for a, cut in enumerate((S // 2, LEAD_COLUMNS)):
+            for cols in (slice(0, cut), slice(cut, S)):
                 nc.vector.tensor_scalar(
                     out_sb[a][:, cols], windows[a][:, cols], s_sb[:, a : a + 1], b_sb[:, a : a + 1], MULT, ADD
                 )

@@ -2,6 +2,7 @@ import concourse.mybir as mybir
 
 BF16, F32, U16 = mybir.dt.bfloat16, mybir.dt.float32, mybir.dt.uint16
 MULT, ADD, IS_EQUAL = mybir.AluOpType.mult, mybir.AluOpType.add, mybir.AluOpType.is_equal
+IDENTITY = mybir.ActivationFunctionType.Identity
 
 P = 128
 E, K, M, S, N = 2, 512, 256, 256, 256
@@ -28,10 +29,10 @@ def tile_scatter_matmul_kernel(tc, base, x, w, s, b, offs, out):
     ):
         base_sb = held.tile([P, A, S], BF16, align_bytes=ROW_ALIGN)
         offsets = held.tile([P, N // 16], U16)
-        x_early = [held.tile([P, HALF, PIECE], BF16, name=f"x_early{e}", align_bytes=ROW_ALIGN) for e in range(E)]
-        x_late = held.tile([P, HALF, N], BF16, align_bytes=ROW_ALIGN)
+        x_sb = held.tile([P, Q, N], BF16, align_bytes=ROW_ALIGN)
         w_first = held.tile([P, Q, M], BF16, align_bytes=ROW_ALIGN)
-        w_second = [held.tile([P, Q, P], BF16, name=f"w_second{a}", align_bytes=ROW_ALIGN) for a in range(A)]
+        w_second_early = held.tile([P, HALF, M], BF16, align_bytes=ROW_ALIGN)
+        w_second_late = [held.tile([P, HALF, P], BF16, name=f"w_second_late{a}", align_bytes=ROW_ALIGN) for a in range(A)]
         s_sb = held.tile([P, A], F32)
         b_sb = held.tile([P, A], F32)
         out_sb = [held.tile([P, S], F32, name=f"out_sb{a}", align_bytes=ROW_ALIGN) for a in range(A)]
@@ -43,26 +44,36 @@ def tile_scatter_matmul_kernel(tc, base, x, w, s, b, offs, out):
         def columns(i):
             return slice(i * P, (i + 1) * P)
 
+        def load_x(blocks):
+            nc.sync.dma_start(x_sb[:, blocks, :], x_blocks[:, blocks, :])
+
         def load_first(blocks):
             nc.sync.dma_start(w_first[:, blocks, :], w_blocks[0, :, blocks, :])
 
+        def load_second_late(a):
+            nc.sync.dma_start(w_second_late[a][:], w_blocks[1, :, HALF:, columns(a)])
+
         nc.sync.dma_start(base_sb[:], base.rearrange("(a p) t -> p a t", p=P))
-        nc.sync.dma_start(offsets[:], offs)
-        nc.sync.dma_start(x_early[0][:], x_blocks[:, :HALF, columns(0)])
+        load_x(slice(0, 1))
         load_first(slice(0, 1))
+        nc.sync.dma_start(offsets[:], offs)
+        nc.sync.dma_start(w_second_early[:], w_blocks[1, :, :HALF, :])
+        load_x(slice(1, HALF))
         load_first(slice(1, Q - 1))
-        nc.sync.dma_start(x_late[:], x_blocks[:, HALF:, :])
+        load_x(slice(HALF, Q))
+        load_second_late(0)
         load_first(slice(Q - 1, Q))
-        nc.sync.dma_start(w_second[0][:], w_blocks[1, :, :, columns(0)])
-        nc.sync.dma_start(x_early[1][:], x_blocks[:, :HALF, columns(1)])
-        nc.sync.dma_start(w_second[1][:], w_blocks[1, :, :, columns(1)])
         nc.sync.dma_start(s_sb[:], s.rearrange("(a p) o -> p (a o)", p=P))
         nc.sync.dma_start(b_sb[:], b.rearrange("(a p) o -> p (a o)", p=P))
+        load_second_late(1)
 
         seed = held.tile([P, 1], F32)
         nc.vector.memset(seed[:], 0.0)
         idle_bank = psum.tile([1, WARM_COLUMNS], F32)
         nc.tensor.matmul(idle_bank[:], seed[:], seed[:].to_broadcast([P, WARM_COLUMNS]))
+
+        idle_column = held.tile([P, 1], F32)
+        nc.scalar.activation(idle_column[:], seed[:], IDENTITY)
 
         distance = held.tile([P, P], F32)
         nc.gpsimd.iota(
@@ -74,28 +85,31 @@ def tile_scatter_matmul_kernel(tc, base, x, w, s, b, offs, out):
         for a in range(A):
             nc.tensor.matmul(windows[a][:], ident[:], base_sb[:, a, :], start=True, stop=False)
 
-        second_order = [*range(HALF, Q), *range(HALF)]
+        def weights(e, a, q):
+            if e == 0:
+                return w_first[:, q, columns(a)]
+            return w_second_early[:, q, columns(a)] if q < HALF else w_second_late[a][:, q - HALF, :]
 
         def scatter(e, a, q, last=False):
             nc.tensor.matmul(
                 windows[a][:].indirect(offsets[:, e * CUT : (e + 1) * CUT]),
-                w_first[:, q, columns(a)] if e == 0 else w_second[a][:, q, :],
-                x_early[e][:, q, :] if q < HALF else x_late[:, q - HALF, columns(e)],
+                weights(e, a, q),
+                x_sb[:, q, columns(e)],
                 start=False,
                 stop=last,
             )
 
-        for q in range(Q):
+        steps = [(e if q % 2 == 0 else E - 1 - e, q) for q in range(Q) for e in range(E)]
+        for e, q in steps[: E * HALF]:
             for a in range(A):
-                scatter(0, a, q)
+                scatter(e, a, q)
         for a in range(A):
-            for q in second_order:
-                scatter(1, a, q, last=(q == second_order[-1]))
+            for e, q in steps[E * HALF :]:
+                scatter(e, a, q, last=((e, q) == steps[-1]))
 
         out_rows = out.rearrange("(a p) t -> p a t", p=P)
-        for a, cut in enumerate((S // 2, LEAD_COLUMNS)):
-            for cols in (slice(0, cut), slice(cut, S)):
-                nc.vector.tensor_scalar(
-                    out_sb[a][:, cols], windows[a][:, cols], s_sb[:, a : a + 1], b_sb[:, a : a + 1], MULT, ADD
-                )
-                nc.sync.dma_start(out_rows[:, a, cols], out_sb[a][:, cols])
+        nc.vector.tensor_scalar(out_sb[0][:], windows[0][:], s_sb[:, 0:1], b_sb[:, 0:1], MULT, ADD)
+        nc.sync.dma_start(out_rows[:, 0, :], out_sb[0][:])
+        for cols in (slice(0, LEAD_COLUMNS), slice(LEAD_COLUMNS, S)):
+            nc.scalar.activation(out_sb[1][:, cols], windows[1][:, cols], IDENTITY, bias=b_sb[:, 1:2], scale=s_sb[:, 1:2])
+            nc.sync.dma_start(out_rows[:, 1, cols], out_sb[1][:, cols])

@@ -30,9 +30,7 @@ def tile_scatter_matmul_kernel(tc, base, x, w, s, b, offs, out):
         base_sb = held.tile([P, A, S], BF16, align_bytes=ROW_ALIGN)
         offsets = held.tile([P, N // 16], U16)
         x_sb = held.tile([P, Q, N], BF16, align_bytes=ROW_ALIGN)
-        w_first = held.tile([P, Q, M], BF16, align_bytes=ROW_ALIGN)
-        w_second_early = held.tile([P, HALF, M], BF16, align_bytes=ROW_ALIGN)
-        w_second_late = [held.tile([P, HALF, P], BF16, name=f"w_second_late{a}", align_bytes=ROW_ALIGN) for a in range(A)]
+        w_sb = held.tile([P, E, Q, M], BF16, align_bytes=ROW_ALIGN)
         s_sb = held.tile([P, A], F32)
         b_sb = held.tile([P, A], F32)
         out_sb = [held.tile([P, S], F32, name=f"out_sb{a}", align_bytes=ROW_ALIGN) for a in range(A)]
@@ -47,25 +45,19 @@ def tile_scatter_matmul_kernel(tc, base, x, w, s, b, offs, out):
         def load_x(blocks):
             nc.sync.dma_start(x_sb[:, blocks, :], x_blocks[:, blocks, :])
 
-        def load_first(blocks):
-            nc.sync.dma_start(w_first[:, blocks, :], w_blocks[0, :, blocks, :])
+        def load_w(e, blocks):
+            nc.sync.dma_start(w_sb[:, e, blocks, :], w_blocks[e, :, blocks, :])
 
-        def load_second_late(a):
-            nc.sync.dma_start(w_second_late[a][:], w_blocks[1, :, HALF:, columns(a)])
-
-        nc.sync.dma_start(base_sb[:], base.rearrange("(a p) t -> p a t", p=P))
+        nc.sync.dma_start(base_sb[:], base.rearrange("(p a) t -> p a t", p=P))
         load_x(slice(0, 1))
-        load_first(slice(0, 1))
+        load_w(0, slice(0, 1))
         nc.sync.dma_start(offsets[:], offs)
-        nc.sync.dma_start(w_second_early[:], w_blocks[1, :, :HALF, :])
-        load_x(slice(1, HALF))
-        load_first(slice(1, Q - 1))
-        load_x(slice(HALF, Q))
-        load_second_late(0)
-        load_first(slice(Q - 1, Q))
-        nc.sync.dma_start(s_sb[:], s.rearrange("(a p) o -> p (a o)", p=P))
-        nc.sync.dma_start(b_sb[:], b.rearrange("(a p) o -> p (a o)", p=P))
-        load_second_late(1)
+        for q in range(1, Q):
+            load_w(q % E, slice(q - 1, q + 1))
+            load_x(slice(q, q + 1))
+        load_w(0, slice(Q - 1, Q))
+        nc.sync.dma_start(s_sb[:], s.rearrange("(p a) o -> p (a o)", p=P))
+        nc.sync.dma_start(b_sb[:], b.rearrange("(p a) o -> p (a o)", p=P))
 
         seed = held.tile([P, 1], F32)
         nc.vector.memset(seed[:], 0.0)
@@ -85,15 +77,10 @@ def tile_scatter_matmul_kernel(tc, base, x, w, s, b, offs, out):
         for a in range(A):
             nc.tensor.matmul(windows[a][:], ident[:], base_sb[:, a, :], start=True, stop=False)
 
-        def weights(e, a, q):
-            if e == 0:
-                return w_first[:, q, columns(a)]
-            return w_second_early[:, q, columns(a)] if q < HALF else w_second_late[a][:, q - HALF, :]
-
         def scatter(e, a, q, last=False):
             nc.tensor.matmul(
                 windows[a][:].indirect(offsets[:, e * CUT : (e + 1) * CUT]),
-                weights(e, a, q),
+                w_sb[:, e, q, a::A],
                 x_sb[:, q, columns(e)],
                 start=False,
                 stop=last,
@@ -107,7 +94,7 @@ def tile_scatter_matmul_kernel(tc, base, x, w, s, b, offs, out):
             for e, q in steps[E * HALF :]:
                 scatter(e, a, q, last=((e, q) == steps[-1]))
 
-        out_rows = out.rearrange("(a p) t -> p a t", p=P)
+        out_rows = out.rearrange("(p a) t -> p a t", p=P)
         nc.vector.tensor_scalar(out_sb[0][:], windows[0][:], s_sb[:, 0:1], b_sb[:, 0:1], MULT, ADD)
         nc.sync.dma_start(out_rows[:, 0, :], out_sb[0][:])
         for cols in (slice(0, LEAD_COLUMNS), slice(LEAD_COLUMNS, S)):

import concourse.mybir as mybir

BF16, F32, U16 = mybir.dt.bfloat16, mybir.dt.float32, mybir.dt.uint16
MULT, ADD, IS_EQUAL = mybir.AluOpType.mult, mybir.AluOpType.add, mybir.AluOpType.is_equal
IDENTITY = mybir.ActivationFunctionType.Identity

P = 128
E, K, M, S, N = 2, 512, 256, 256, 256
PIECE = N // E
CUT = PIECE // 16
Q = K // P
A = M // P
HALF = Q // 2
LEAD_COLUMNS = 64

ROW_ALIGN = 512

WARM_COLUMNS = 320

FLOPS = 2 * N * K * M
BYTES = 2 * (M * S + K * N + E * K * M) + 4 * (M * S + 2 * M) + 2 * P * N // 16


def tile_scatter_matmul_kernel(tc, base, x, w, s, b, offs, out):
    nc = tc.nc
    with (
        tc.tile_pool(name="held", bufs=1) as held,
        tc.psum_pool(name="psum", bufs=1) as psum,
    ):
        base_sb = held.tile([P, A, S], BF16, align_bytes=ROW_ALIGN)
        offsets = held.tile([P, N // 16], U16)
        x_sb = held.tile([P, Q, N], BF16, align_bytes=ROW_ALIGN)
        w_sb = held.tile([P, E, Q, M], BF16, align_bytes=ROW_ALIGN)
        s_sb = held.tile([P, A], F32)
        b_sb = held.tile([P, A], F32)
        out_sb = [held.tile([P, S], F32, name=f"out_sb{a}", align_bytes=ROW_ALIGN) for a in range(A)]
        ident = held.tile([P, P], BF16)

        x_blocks = x.rearrange("(p q) n -> p q n", p=P)
        w_blocks = w.rearrange("e (p q) m -> e p q m", p=P)

        def columns(i):
            return slice(i * P, (i + 1) * P)

        def load_x(blocks):
            nc.sync.dma_start(x_sb[:, blocks, :], x_blocks[:, blocks, :])

        def load_w(e, blocks):
            nc.sync.dma_start(w_sb[:, e, blocks, :], w_blocks[e, :, blocks, :])

        nc.sync.dma_start(base_sb[:], base.rearrange("(p a) t -> p a t", p=P))
        load_x(slice(0, 1))
        load_w(0, slice(0, 1))
        nc.sync.dma_start(offsets[:], offs)
        for q in range(1, Q):
            load_w(q % E, slice(q - 1, q + 1))
            load_x(slice(q, q + 1))
        load_w(0, slice(Q - 1, Q))
        nc.sync.dma_start(s_sb[:], s.rearrange("(p a) o -> p (a o)", p=P))
        nc.sync.dma_start(b_sb[:], b.rearrange("(p a) o -> p (a o)", p=P))

        seed = held.tile([P, 1], F32)
        nc.vector.memset(seed[:], 0.0)
        idle_bank = psum.tile([1, WARM_COLUMNS], F32)
        nc.tensor.matmul(idle_bank[:], seed[:], seed[:].to_broadcast([P, WARM_COLUMNS]))

        idle_column = held.tile([P, 1], F32)
        nc.scalar.activation(idle_column[:], seed[:], IDENTITY)

        distance = held.tile([P, P], F32)
        nc.gpsimd.iota(
            distance[:], pattern=[[1, P]], base=0, channel_multiplier=-1, allow_small_or_imprecise_dtypes=True
        )
        nc.vector.tensor_scalar(ident[:], distance[:], 0.0, None, IS_EQUAL)

        windows = [psum.tile([P, S], F32, name=f"window{a}") for a in range(A)]
        for a in range(A):
            nc.tensor.matmul(windows[a][:], ident[:], base_sb[:, a, :], start=True, stop=False)

        def scatter(e, a, q, last=False):
            nc.tensor.matmul(
                windows[a][:].indirect(offsets[:, e * CUT : (e + 1) * CUT]),
                w_sb[:, e, q, a::A],
                x_sb[:, q, columns(e)],
                start=False,
                stop=last,
            )

        steps = [(e if q % 2 == 0 else E - 1 - e, q) for q in range(Q) for e in range(E)]
        for e, q in steps[: E * HALF]:
            for a in range(A):
                scatter(e, a, q)
        for a in range(A):
            for e, q in steps[E * HALF :]:
                scatter(e, a, q, last=((e, q) == steps[-1]))

        out_rows = out.rearrange("(p a) t -> p a t", p=P)
        nc.vector.tensor_scalar(out_sb[0][:], windows[0][:], s_sb[:, 0:1], b_sb[:, 0:1], MULT, ADD)
        nc.sync.dma_start(out_rows[:, 0, :], out_sb[0][:])
        for cols in (slice(0, LEAD_COLUMNS), slice(LEAD_COLUMNS, S)):
            nc.scalar.activation(out_sb[1][:, cols], windows[1][:, cols], IDENTITY, bias=b_sb[:, 1:2], scale=s_sb[:, 1:2])
            nc.sync.dma_start(out_rows[:, 1, cols], out_sb[1][:, cols])
